import numpy as np
import ml_dtypes


def mxq(x, axis, fmt="e4m3"):
    dtype, down = {"e4m3": (ml_dtypes.float8_e4m3fn, 7), "e5m2": (ml_dtypes.float8_e5m2, 14)}[fmt]
    v = np.moveaxis(np.asarray(x, np.float32).astype(ml_dtypes.bfloat16).astype(np.float64), axis, -1)
    blocks = v.reshape(v.shape[:-1] + (-1, 32))
    amax = np.abs(blocks).max(-1, keepdims=True)
    byte = np.maximum(np.where(amax > 0, np.frexp(amax)[1] - 1 + 127, 0) - down, 1)
    scale = np.exp2(byte - 127.0)
    codes = (blocks / scale).astype(np.float32).astype(dtype).astype(np.float64)
    return np.moveaxis((codes * scale).reshape(v.shape), -1, axis)


WIDE = False


def mx_kscale(k):
    if not WIDE:
        return np.ones(k)
    levels = np.array([10, -10, 5, -5, 0])
    if k % 512:
        return np.exp2(np.random.permutation(np.resize(levels, k // 32))).repeat(32)
    a = np.empty((k // 512, 16))
    for p in range(k // 512):
        a[p, :8] = np.random.permutation(np.resize(levels, 8))
        for g in range(8):
            far = levels[np.abs(levels - a[p, g]) >= 10]
            a[p, g + 8] = far[np.random.randint(len(far))]
    return np.exp2(a.ravel()).repeat(32)


def f64(x):
    return np.asarray(x).astype(np.float64)


def striped(idx):
    return np.tile(idx.reshape(-1, 16).T, (8, 1)).astype(np.uint16)


def unstriped(offs):
    return offs[:16].T.reshape(-1).astype(np.int64)


def striped8(idx):
    return np.concatenate([x.reshape(-1, 16).T for x in idx]).astype(np.uint16)


def runs(offs, k):
    lists = np.stack([offs[16 * r : 16 * r + 16].T.reshape(-1) for r in range(8)]).astype(np.int64)
    return lists[np.arange(k) % 512 // 64]


def pack_weight(w):
    k, n = w.shape
    w = f64(np.asarray(w, np.float32).astype(ml_dtypes.bfloat16)).reshape(k // 32, 32, n)
    amax = np.abs(w).max(1)
    byte = np.clip(np.where(amax > 0, np.frexp(amax)[1] - 1 + 127 - 7, 1), 1, 254)
    scaled = (w * np.exp2(127.0 - byte)[:, None, :]).reshape(k, n).astype(np.float32)
    words = np.ascontiguousarray(scaled.reshape(k // 512, 128, 4, n).transpose(0, 1, 3, 2)).astype(ml_dtypes.float8_e4m3fn).view(np.uint8)
    return words, np.ascontiguousarray(byte.astype(np.uint8).reshape(k // 512, 16, n))


def unpack_weight(words, scales):
    g, p, n, _ = words.shape
    vals = np.ascontiguousarray(words).view(ml_dtypes.float8_e4m3fn).astype(np.float64) * np.repeat(np.exp2(scales.astype(np.float64) - 127.0), 8, axis=1)[..., None]
    return vals.transpose(0, 1, 3, 2).reshape(g * 512, n)

def planes(y):
    n, m = y.shape
    v = y.astype(np.float32).astype(ml_dtypes.bfloat16).astype(np.float64).reshape(n // 32, 32, m)
    top = np.abs(v).max(1)
    byte = np.clip(np.where(top > 0, np.frexp(top)[1] - 1 + 127 - 7, 1), 1, 254)
    codes = (v * np.exp2(127.0 - byte)[:, None, :]).reshape(n, m).astype(np.float32).astype(ml_dtypes.float8_e4m3fn).view(np.uint8)
    words = codes.reshape(n // 512, 128, 4, m).transpose(0, 1, 3, 2)
    return np.ascontiguousarray(words), np.ascontiguousarray(byte.astype(np.uint8).reshape(n // 512, 16, m))


K, T, S, N, H, U = 512, 2048, 512, 512, 512, 1024


def setup_inputs():
    n = np.random.standard_normal
    s = mx_kscale(K)[:, None]
    u = mx_kscale(H)
    packed_xT = pack_weight(n((K, T)) * s)
    packed_w1 = pack_weight(n((K, H)) / np.sqrt(K) / s)
    packed_w2 = pack_weight(n((K, H)) / np.sqrt(K) / s)
    packed_w3 = pack_weight(n((H, N)) / np.sqrt(H) / u[:, None])
    return {
        "x_words": packed_xT[0],
        "x_scales": packed_xT[1],
        "w1_words": packed_w1[0],
        "w1_scales": packed_w1[1],
        "w2_words": packed_w2[0],
        "w2_scales": packed_w2[1],
        "gn": (np.random.uniform(0.5, 1.5, (H, 1)) * u[:, None]).astype(np.float32),
        "w3_words": packed_w3[0],
        "w3_scales": packed_w3[1],
        "mem": n((N, U)).astype(np.float32),
        "offs": striped(np.random.permutation(T)[:S]),
        "two": striped(np.random.permutation(T)[:S]),
        "n1": striped8(np.stack([np.random.permutation(S) for _ in range(8)])),
        "n2": striped8(np.stack([np.random.permutation(S) for _ in range(8)])),
        "slot": striped8(np.stack([np.random.permutation(U)[:S] for _ in range(8)])),
    }


def reference(x_words, x_scales, w1_words, w1_scales, w2_words, w2_scales, gn, w3_words, w3_scales, mem, offs, two, n1, n2, slot):
    xq = unpack_weight(x_words, x_scales)[:, unstriped(offs)]
    y = unpack_weight(w1_words, w1_scales).T @ xq
    p = np.maximum(y, y[np.arange(H)[:, None], runs(n1, H)])
    x_two = unpack_weight(x_words, x_scales)[:, unstriped(two)]
    c = unpack_weight(w2_words, w2_scales).T @ x_two
    qv = np.minimum(c, c[np.arange(H)[:, None], runs(n2, H)])
    z = f64(gn) * (p * (qv[np.arange(H)[:, None], runs(n1, H)]) - (qv * (p[np.arange(H)[:, None], runs(n2, H)])))
    h = unpack_weight(w3_words, w3_scales).T @ mxq(z, 0, "e4m3")
    out = f64(mem).copy()
    out[np.arange(N)[:, None], runs(slot, N)] = h
    return (out,) + planes(out)

@@ -1,0 +1,226 @@
+from contextlib import ExitStack
+
+import concourse.mybir as mybir
+
+F32 = mybir.dt.float32
+BF16 = mybir.dt.bfloat16
+I32 = mybir.dt.int32
+U32 = mybir.dt.uint32
+U16 = mybir.dt.uint16
+U8 = mybir.dt.uint8
+FP8X4 = mybir.dt.float8_e4m3fn_x4
+ALU = mybir.AluOpType
+COPY = mybir.ActivationFunctionType.Copy
+
+P = 128
+PACK = 4
+K, T, S, N, H, U = 512, 2048, 512, 512, 512, 1024
+LIST_ROWS = 16
+HALF = S // 2
+CHUNKS = ((0, 128), (128, 256), (256, 512))
+OUT_CHUNK = 256
+FLOPS = 2 * (K * H * S * 2 + H * N * S)
+
+
+def entries(offsets, lo, hi):
+    return offsets[:, lo // LIST_ROWS : hi // LIST_ROWS]
+
+
+def load_scale_rows(queue, plane, scales):
+    for q in range(4):
+        rows = scales[0, 4 * q : 4 * q + 4, :].bitcast(I32)
+        queue.dma_start(out=plane[32 * q : 32 * q + 32, :].bitcast(I32),
+                        in_=rows.unsqueeze(0).to_broadcast([8, 4, rows.shape[1]]))
+
+
+def words_of(packed):
+    return packed[0].rearrange("p c r -> p (c r)").bitcast(I32)
+
+
+def tile_picked_wedge2_none_po_kernel(
+    tc, x_words, x_scales, w1_words, w1_scales, w2_words, w2_scales, gn, w3_words, w3_scales, mem,
+    offs, two, n1, n2, slot, out_0, out_1, out_2,
+):
+    nc = tc.nc
+    with ExitStack() as ctx:
+        lists = ctx.enter_context(tc.tile_pool(name="lists", bufs=1))
+        keep = ctx.enter_context(tc.tile_pool(name="keep", bufs=1))
+        psum = ctx.enter_context(tc.psum_pool(name="psum", bufs=1))
+
+        offs_t = lists.tile([P, S // LIST_ROWS], U16, name="offs_t")
+        two_t = lists.tile([P, S // LIST_ROWS], U16, name="two_t")
+        n1_t = lists.tile([P, S // LIST_ROWS], U16, name="n1_t")
+        n2_t = lists.tile([P, S // LIST_ROWS], U16, name="n2_t")
+        slot_t = lists.tile([P, S // LIST_ROWS], U16, name="slot_t")
+
+        x_plane = keep.tile([P, T], U8, name="x_plane", align_bytes=64)
+        x_codes = keep.tile([P, T], I32, name="x_codes", align_bytes=64)
+        w_plane = [keep.tile([P, H], U8, name=f"w_plane{i}", align_bytes=64) for i in range(3)]
+        wd_plane = [keep.tile([P, H], U8, name=f"wd_plane{i}", align_bytes=64) for i in range(3)]
+        wd_codes = [keep.tile([P, H], U32, name=f"wd_codes{i}", align_bytes=64) for i in range(3)]
+        gain = keep.tile([P, PACK], F32, name="gain")
+        minus_gain = keep.tile([P, PACK], F32, name="minus_gain")
+
+
+        def load_codes(words, i):
+            codes = keep.tile([P, H], I32, name=f"w_codes{i}", align_bytes=64)
+            nc.sync.dma_start(out=codes[:], in_=words_of(words))
+            return codes
+
+        def deal_plane(i):
+            nc.gpsimd.tensor_copy(out=wd_plane[i][:].rearrange("p (t m) -> p t m", t=PACK),
+                                  in_=w_plane[i][:].rearrange("p (m t) -> p t m", t=PACK))
+
+        def deal_codes(copy, i, codes):
+            copy(out=wd_codes[i][:].rearrange("p (t m) -> p t m", t=PACK),
+                 in_=codes[:].bitcast(U32).rearrange("p (m t) -> p t m", t=PACK))
+
+        nc.sync.dma_start(offs_t[:], offs)
+        load_scale_rows(nc.sync, x_plane, x_scales)
+        nc.sync.dma_start(out=x_codes[:], in_=words_of(x_words))
+        nc.sync.dma_start(two_t[:], two)
+        w1_codes = load_codes(w1_words, 0)
+        load_scale_rows(nc.sync, w_plane[0], w1_scales)
+        nc.gpsimd.dma_start(out=gain[:], in_=gn.rearrange("(p t) o -> p (t o)", t=PACK))
+        nc.scalar.activation(minus_gain[:], gain[:], COPY, scale=-1.0)
+        nc.sync.dma_start(n1_t[:], n1)
+        w2_codes = load_codes(w2_words, 1)
+        load_scale_rows(nc.sync, w_plane[1], w2_scales)
+        nc.sync.dma_start(n2_t[:], n2)
+        nc.sync.dma_start(slot_t[:], slot)
+        w3_codes = load_codes(w3_words, 2)
+        load_scale_rows(nc.sync, w_plane[2], w3_scales)
+        deal_plane(0)
+        deal_codes(nc.scalar.copy, 0, w1_codes)
+        deal_plane(1)
+        deal_codes(nc.scalar.copy, 1, w2_codes)
+        deal_plane(2)
+        deal_codes(nc.gpsimd.tensor_copy, 2, w3_codes)
+
+        picked_plane = [keep.tile([P, S], U8, name=f"picked_plane{i}", align_bytes=64) for i in range(2)]
+        picked_codes = [keep.tile([P, S], U32, name=f"picked_codes{i}", align_bytes=64) for i in range(2)]
+        for i, offsets in enumerate((offs_t, two_t)):
+            nc.vector.tensor_copy(picked_plane[i][:], x_plane[:].indirect(offsets[:]))
+            nc.vector.tensor_copy(picked_codes[i][:], x_codes[:].bitcast(U32).indirect(offsets[:]))
+
+        mem_rows = mem.rearrange("(p t) w -> p t w", t=PACK)
+
+        def product(bank, i, t, codes, plane):
+            cols = slice(P * t, P * (t + 1))
+            nc.tensor.matmul_mx(out=bank, lhsT=wd_codes[i][:, cols].bitcast(FP8X4), lhsT_scale=wd_plane[i][:, cols],
+                                rhs=codes.bitcast(FP8X4), rhs_scale=plane, start=True, stop=True)
+
+        y_bank = [psum.tile([P, S], F32, name=f"y_bank{t}", tag=f"bank{t}") for t in range(PACK)]
+        c_bank = [psum.tile([P, S], F32, name=f"c_bank{t}", tag=f"bank{PACK + t}") for t in range(PACK)]
+        y = [keep.tile([P, S], F32, name=f"y{t}", align_bytes=64) for t in range(PACK)]
+        c = [keep.tile([P, S], F32, name=f"c{t}", align_bytes=64) for t in range(PACK)]
+        y_at = [keep.tile([P, S], F32, name=f"y_at{t}", align_bytes=64) for t in range(PACK)]
+        c_at = [keep.tile([P, S], F32, name=f"c_at{t}", align_bytes=64) for t in range(PACK)]
+        pmax = [keep.tile([P, S], F32, name=f"pmax{t}", align_bytes=64) for t in range(PACK)]
+        qmin = [keep.tile([P, S], F32, name=f"qmin{t}", align_bytes=64) for t in range(PACK)]
+
+        for t in range(PACK):
+            product(y_bank[t][:], 0, t, picked_codes[0][:], picked_plane[0][:])
+        for t in range(PACK):
+            product(c_bank[t][:], 1, t, picked_codes[1][:], picked_plane[1][:])
+        page = []
+        for t, tag in enumerate(("x_plane", "picked_codes0", "x_codes", "picked_codes1")):
+            page.append(keep.tile([P, U], F32, name=f"page{t}", tag=tag, align_bytes=64))
+            nc.sync.dma_start(out=page[t][:], in_=mem_rows[:, t, :])
+        for t in range(PACK):
+            nc.scalar.copy(out=y[t][:], in_=y_bank[t][:])
+        for t in range(PACK):
+            for lo in (0, HALF):
+                nc.vector.tensor_copy(y_at[t][:, lo : lo + HALF], y[t][:].indirect(entries(n1_t, lo, lo + HALF)))
+            nc.vector.tensor_tensor(out=pmax[t][:], in0=y_at[t][:], in1=y_bank[t][:], op=ALU.max)
+        for t in range(PACK):
+            nc.scalar.copy(out=c[t][:], in_=c_bank[t][:])
+            for lo in (0, HALF):
+                nc.scalar.activation(c_at[t][:, lo : lo + HALF], c[t][:].indirect(entries(n2_t, lo, lo + HALF)), COPY)
+
+        def fetch(engine, j, name, source, offsets, tag):
+            lo, hi = CHUNKS[j]
+            fetched = keep.tile([P, PACK, hi - lo], F32, name=f"{name}{j}", tag=tag, align_bytes=64)
+            for t in range(PACK):
+                window = source[t][:].indirect(entries(offsets, lo, hi))
+                if engine == "scalar":
+                    nc.scalar.activation(fetched[:, t, :], window, COPY)
+                else:
+                    nc.vector.tensor_copy(fetched[:, t, :], window)
+            return fetched
+
+        def second_stage(j, p_at, q_at, tags):
+            lo, hi = CHUNKS[j]
+            n = hi - lo
+            right = keep.tile([P, PACK, n], F32, name=f"right{j}", tag=tags[0], align_bytes=64)
+            left = keep.tile([P, PACK, n], F32, name=f"left{j}", tag=tags[1], align_bytes=64)
+            z = keep.tile([P, n, PACK], BF16, name=f"z{j}", align_bytes=64)
+            z_codes = keep.tile([P, n], U32, name=f"z_codes{j}", align_bytes=64)
+            z_plane = keep.tile([P, n], U8, name=f"z_plane{j}", align_bytes=64)
+            for t in range(PACK):
+                nc.vector.scalar_tensor_tensor(out=right[:, t, :], in0=qmin[t][:, lo:hi], scalar=minus_gain[:, t : t + 1],
+                                               in1=p_at[:, t, :], op0=ALU.mult, op1=ALU.mult)
+            for t in range(PACK):
+                nc.vector.scalar_tensor_tensor(out=left[:, t, :], in0=pmax[t][:, lo:hi], scalar=gain[:, t : t + 1],
+                                               in1=q_at[:, t, :], op0=ALU.mult, op1=ALU.mult)
+            nc.vector.tensor_tensor(out=z[:].rearrange("p (a i) t -> p a t i", i=4),
+                                    in0=left[:].rearrange("p t (a i) -> p a t i", i=4),
+                                    in1=right[:].rearrange("p t (a i) -> p a t i", i=4), op=ALU.add)
+            nc.vector.quantize_mx(out=z_codes[:].bitcast(FP8X4), scales=z_plane[:], in_=z[:].rearrange("p c t -> p (c t)"))
+            halves = []
+            per_bank = S // n
+            for b in range(PACK // per_bank):
+                bank = psum.tile([P, per_bank, n], F32, name=f"h_bank{j}_{b}", tag=f"bank{j + b}")
+                for u in range(per_bank):
+                    product(bank[:, u, :], 2, b * per_bank + u, z_codes[:], z_plane[:])
+                for u in range(0, per_bank, 2):
+                    half = keep.tile([P, 2, n], F32, name=f"h{j}_{len(halves)}", align_bytes=64)
+                    nc.scalar.copy(out=half[:], in_=bank[:, u : u + 2, :])
+                    halves.append(half)
+            return halves
+
+        def scatter(j, t):
+            lo, hi = CHUNKS[j]
+            nc.vector.tensor_copy(page[t][:].indirect(entries(slot_t, lo, hi)), h[j][t // 2][:, t % 2, :])
+
+        h = []
+        p_at0 = fetch("vector", 0, "p_at", pmax, n2_t, "p_at0")
+        for t in range(PACK):
+            nc.vector.tensor_tensor(out=qmin[t][:], in0=c_at[t][:], in1=c_bank[t][:], op=ALU.min)
+        q_at0 = fetch("scalar", 0, "q_at", qmin, n1_t, "q_at0")
+        h.append(second_stage(0, p_at0, q_at0, ("right0", "left0")))
+        p_at1 = fetch("vector", 1, "p_at", pmax, n2_t, "right0")
+        q_at1 = fetch("scalar", 1, "q_at", qmin, n1_t, "q_at1")
+        h.append(second_stage(1, p_at1, q_at1, ("right1", "left1")))
+        p_at2 = fetch("scalar", 2, "p_at", pmax, n2_t, "z_codes0")
+        q_at2 = fetch("scalar", 2, "q_at", qmin, n1_t, "z_plane0")
+        for t in range(PACK):
+            scatter(0, t)
+        for t in range(2):
+            scatter(1, t)
+        h.append(second_stage(2, p_at2, q_at2, ("h1_0", "h0_1")))
+        for t in range(2, PACK):
+            scatter(1, t)
+        out_rows = out_0.rearrange("(p t) w -> p t w", t=PACK)
+        for t in range(PACK):
+            scatter(2, t)
+            nc.sync.dma_start(out=out_rows[:, t, :], in_=page[t][:])
+
+        out_plane = keep.tile([P, U], U8, name="out_plane", align_bytes=64)
+        out_words = words_of(out_1)
+        blocks = U // OUT_CHUNK
+        pairs = [keep.tile([P, 2, OUT_CHUNK, 2], BF16, name=f"pairs{b}", align_bytes=64) for b in range(blocks)]
+        for t in range(PACK):
+            for b in range(blocks):
+                nc.scalar.copy(out=pairs[b][:, t // 2, :, t % 2], in_=page[t][:, b * OUT_CHUNK : (b + 1) * OUT_CHUNK])
+        for b in range(blocks):
+            cols = slice(b * OUT_CHUNK, (b + 1) * OUT_CHUNK)
+            grouped = keep.tile([P, OUT_CHUNK * PACK], BF16, name=f"grouped{b}", align_bytes=64)
+            out_codes = keep.tile([P, OUT_CHUNK], I32, name=f"out_codes{b}", align_bytes=64)
+            weave = nc.scalar.copy if b == blocks - 1 else nc.vector.tensor_copy
+            weave(out=grouped[:].bitcast(F32).rearrange("p (a i u) -> p a u i", i=4, u=2),
+                  in_=pairs[b][:].rearrange("p u c e -> p (u c e)").bitcast(F32).rearrange("p (u a i) -> p a u i", u=2, i=4))
+            nc.vector.quantize_mx(out=out_codes[:].bitcast(FP8X4), scales=out_plane[:, cols], in_=grouped[:])
+            nc.sync.dma_start(out=out_words[:, cols], in_=out_codes[:])
+        for q in range(4):
+            nc.scalar.dma_start(out=out_2[0, 4 * q : 4 * q + 4, :].bitcast(I32), in_=out_plane[32 * q : 32 * q + 4, :].bitcast(I32))

@@ -18,6 +18,7 @@ K, T, S, N, H, U = 512, 2048, 512, 512, 512, 1024
 LIST_ROWS = 16
 HALF = S // 2
 CHUNKS = ((0, 128), (128, 256), (256, 512))
+PIECE = 128
 OUT_CHUNK = 256
 FLOPS = 2 * (K * H * S * 2 + H * N * S)
 
@@ -26,15 +27,25 @@ def entries(offsets, lo, hi):
     return offsets[:, lo // LIST_ROWS : hi // LIST_ROWS]
 
 
-def load_scale_rows(queue, plane, scales):
+def load_scale_rows_repeated(nc, plane, scales):
     for q in range(4):
         rows = scales[0, 4 * q : 4 * q + 4, :].bitcast(I32)
-        queue.dma_start(out=plane[32 * q : 32 * q + 32, :].bitcast(I32),
-                        in_=rows.unsqueeze(0).to_broadcast([8, 4, rows.shape[1]]))
+        nc.sync.dma_start(out=plane[32 * q : 32 * q + 32, :].bitcast(I32),
+                          in_=rows.unsqueeze(0).to_broadcast([8, 4, rows.shape[1]]))
+
+
+def load_scale_rows(nc, plane, first, scales):
+    for q in range(4):
+        nc.sync.dma_start(out=plane[32 * q + first : 32 * q + first + 4, :].bitcast(I32),
+                          in_=scales[0, 4 * q : 4 * q + 4, :].bitcast(I32))
 
 
 def words_of(packed):
     return packed[0].rearrange("p c r -> p (c r)").bitcast(I32)
+
+
+def deal_columns(copy, dealt, natural):
+    copy(out=dealt.rearrange("p (t m) -> p t m", t=PACK), in_=natural.rearrange("p (m t) -> p t m", t=PACK))
 
 
 def tile_picked_wedge2_none_po_kernel(
@@ -47,180 +58,222 @@ def tile_picked_wedge2_none_po_kernel(
         keep = ctx.enter_context(tc.tile_pool(name="keep", bufs=1))
         psum = ctx.enter_context(tc.psum_pool(name="psum", bufs=1))
 
+        def sbuf(name, shape, dtype, tag=None):
+            return keep.tile([P] + shape, dtype, name=name, tag=tag or name, align_bytes=64)
+
         offs_t = lists.tile([P, S // LIST_ROWS], U16, name="offs_t")
         two_t = lists.tile([P, S // LIST_ROWS], U16, name="two_t")
         n1_t = lists.tile([P, S // LIST_ROWS], U16, name="n1_t")
         n2_t = lists.tile([P, S // LIST_ROWS], U16, name="n2_t")
         slot_t = lists.tile([P, S // LIST_ROWS], U16, name="slot_t")
 
-        x_plane = keep.tile([P, T], U8, name="x_plane", align_bytes=64)
-        x_codes = keep.tile([P, T], I32, name="x_codes", align_bytes=64)
-        w_plane = [keep.tile([P, H], U8, name=f"w_plane{i}", align_bytes=64) for i in range(3)]
-        wd_plane = [keep.tile([P, H], U8, name=f"wd_plane{i}", align_bytes=64) for i in range(3)]
-        wd_codes = [keep.tile([P, H], U32, name=f"wd_codes{i}", align_bytes=64) for i in range(3)]
+        x_plane = sbuf("x_plane", [T], U8)
+        x_codes = sbuf("x_codes", [T], I32)
+        w1_plane = sbuf("w1_plane", [H], U8)
+        w23_plane = sbuf("w23_plane", [H], U8)
+        w1_dealt_plane = sbuf("w1_dealt_plane", [H], U8)
+        w23_dealt_plane = sbuf("w23_dealt_plane", [H], U8)
+        w_codes = [sbuf(f"w_codes{i}", [H], I32) for i in range(3)]
+        dealt_codes = [sbuf(f"dealt_codes{i}", [H], U32) for i in range(3)]
+        dealt_planes = [w1_dealt_plane[:], w23_dealt_plane[:], w23_dealt_plane[4:P, :]]
         gain = keep.tile([P, PACK], F32, name="gain")
         minus_gain = keep.tile([P, PACK], F32, name="minus_gain")
 
-
-        def load_codes(words, i):
-            codes = keep.tile([P, H], I32, name=f"w_codes{i}", align_bytes=64)
-            nc.sync.dma_start(out=codes[:], in_=words_of(words))
-            return codes
-
-        def deal_plane(i):
-            nc.gpsimd.tensor_copy(out=wd_plane[i][:].rearrange("p (t m) -> p t m", t=PACK),
-                                  in_=w_plane[i][:].rearrange("p (m t) -> p t m", t=PACK))
-
-        def deal_codes(copy, i, codes):
-            copy(out=wd_codes[i][:].rearrange("p (t m) -> p t m", t=PACK),
-                 in_=codes[:].bitcast(U32).rearrange("p (m t) -> p t m", t=PACK))
-
-        nc.sync.dma_start(offs_t[:], offs)
-        load_scale_rows(nc.sync, x_plane, x_scales)
-        nc.sync.dma_start(out=x_codes[:], in_=words_of(x_words))
-        nc.sync.dma_start(two_t[:], two)
-        w1_codes = load_codes(w1_words, 0)
-        load_scale_rows(nc.sync, w_plane[0], w1_scales)
+        nc.vector.memset(w23_plane[:].bitcast(I32), 0)
         nc.gpsimd.dma_start(out=gain[:], in_=gn.rearrange("(p t) o -> p (t o)", t=PACK))
         nc.scalar.activation(minus_gain[:], gain[:], COPY, scale=-1.0)
+        nc.sync.dma_start(offs_t[:], offs)
+        load_scale_rows_repeated(nc, x_plane, x_scales)
+        nc.sync.dma_start(two_t[:], two)
+        nc.sync.dma_start(out=x_codes[:], in_=words_of(x_words))
+        nc.sync.dma_start(out=w_codes[0][:], in_=words_of(w1_words))
+        load_scale_rows_repeated(nc, w1_plane, w1_scales)
+        load_scale_rows(nc, w23_plane, 0, w2_scales)
+        load_scale_rows(nc, w23_plane, 4, w3_scales)
+        nc.sync.dma_start(out=w_codes[1][:], in_=words_of(w2_words))
         nc.sync.dma_start(n1_t[:], n1)
-        w2_codes = load_codes(w2_words, 1)
-        load_scale_rows(nc.sync, w_plane[1], w2_scales)
         nc.sync.dma_start(n2_t[:], n2)
+        nc.sync.dma_start(out=w_codes[2][:], in_=words_of(w3_words))
         nc.sync.dma_start(slot_t[:], slot)
-        w3_codes = load_codes(w3_words, 2)
-        load_scale_rows(nc.sync, w_plane[2], w3_scales)
-        deal_plane(0)
-        deal_codes(nc.scalar.copy, 0, w1_codes)
-        deal_plane(1)
-        deal_codes(nc.scalar.copy, 1, w2_codes)
-        deal_plane(2)
-        deal_codes(nc.gpsimd.tensor_copy, 2, w3_codes)
+        for i in range(2):
+            deal_columns(nc.scalar.copy, dealt_codes[i][:], w_codes[i][:].bitcast(U32))
 
-        picked_plane = [keep.tile([P, S], U8, name=f"picked_plane{i}", align_bytes=64) for i in range(2)]
-        picked_codes = [keep.tile([P, S], U32, name=f"picked_codes{i}", align_bytes=64) for i in range(2)]
+        picked_plane = [sbuf(f"picked_plane{i}", [S], U8) for i in range(2)]
+        picked_codes = []
         for i, offsets in enumerate((offs_t, two_t)):
             nc.vector.tensor_copy(picked_plane[i][:], x_plane[:].indirect(offsets[:]))
+        for i, offsets in enumerate((offs_t, two_t)):
+            picked_codes.append(sbuf(f"picked_codes{i}", [S], U32, "w1_plane" if i else None))
             nc.vector.tensor_copy(picked_codes[i][:], x_codes[:].bitcast(U32).indirect(offsets[:]))
-
-        mem_rows = mem.rearrange("(p t) w -> p t w", t=PACK)
+            deal_columns(nc.vector.tensor_copy, (w1_dealt_plane, w23_dealt_plane)[i][:], (w1_plane, w23_plane)[i][:])
 
         def product(bank, i, t, codes, plane):
             cols = slice(P * t, P * (t + 1))
-            nc.tensor.matmul_mx(out=bank, lhsT=wd_codes[i][:, cols].bitcast(FP8X4), lhsT_scale=wd_plane[i][:, cols],
+            nc.tensor.matmul_mx(out=bank, lhsT=dealt_codes[i][:, cols].bitcast(FP8X4), lhsT_scale=dealt_planes[i][:, cols],
                                 rhs=codes.bitcast(FP8X4), rhs_scale=plane, start=True, stop=True)
 
         y_bank = [psum.tile([P, S], F32, name=f"y_bank{t}", tag=f"bank{t}") for t in range(PACK)]
         c_bank = [psum.tile([P, S], F32, name=f"c_bank{t}", tag=f"bank{PACK + t}") for t in range(PACK)]
-        y = [keep.tile([P, S], F32, name=f"y{t}", align_bytes=64) for t in range(PACK)]
-        c = [keep.tile([P, S], F32, name=f"c{t}", align_bytes=64) for t in range(PACK)]
-        y_at = [keep.tile([P, S], F32, name=f"y_at{t}", align_bytes=64) for t in range(PACK)]
-        c_at = [keep.tile([P, S], F32, name=f"c_at{t}", align_bytes=64) for t in range(PACK)]
-        pmax = [keep.tile([P, S], F32, name=f"pmax{t}", align_bytes=64) for t in range(PACK)]
-        qmin = [keep.tile([P, S], F32, name=f"qmin{t}", align_bytes=64) for t in range(PACK)]
+        y = [sbuf(f"y{t}", [S], F32) for t in range(PACK)]
+        c_at = [sbuf(f"c_at{t}", [S], F32) for t in range(PACK)]
+        pmax = [sbuf(f"pmax{t}", [S], F32) for t in range(PACK)]
+        qmin = [sbuf(f"qmin{t}", [S], F32) for t in range(PACK)]
 
         for t in range(PACK):
             product(y_bank[t][:], 0, t, picked_codes[0][:], picked_plane[0][:])
         for t in range(PACK):
             product(c_bank[t][:], 1, t, picked_codes[1][:], picked_plane[1][:])
+        mem_rows = mem.rearrange("(p t) w -> p t w", t=PACK)
         page = []
-        for t, tag in enumerate(("x_plane", "picked_codes0", "x_codes", "picked_codes1")):
-            page.append(keep.tile([P, U], F32, name=f"page{t}", tag=tag, align_bytes=64))
+        for t, tag in enumerate(("x_plane", "picked_codes0", "x_codes", "w1_plane")):
+            page.append(sbuf(f"page{t}", [U], F32, tag))
             nc.sync.dma_start(out=page[t][:], in_=mem_rows[:, t, :])
+
+        def gather(engine, out, source, offsets, lo, hi):
+            window = source[:].indirect(entries(offsets, lo, hi))
+            if engine == "scalar":
+                nc.scalar.activation(out, window, COPY)
+            else:
+                nc.vector.tensor_copy(out, window)
+
         for t in range(PACK):
             nc.scalar.copy(out=y[t][:], in_=y_bank[t][:])
+        c = []
         for t in range(PACK):
+            c.append(sbuf(f"c{t}", [2 * S], F32, f"y{t - 1}" if t else "w23_plane"))
+            y_at = c[t][:, S:]
             for lo in (0, HALF):
-                nc.vector.tensor_copy(y_at[t][:, lo : lo + HALF], y[t][:].indirect(entries(n1_t, lo, lo + HALF)))
-            nc.vector.tensor_tensor(out=pmax[t][:], in0=y_at[t][:], in1=y_bank[t][:], op=ALU.max)
+                gather("vector", y_at[:, lo : lo + HALF], y[t], n1_t, lo, lo + HALF)
+            for lo in (0, HALF):
+                cols = slice(lo, lo + HALF)
+                nc.vector.tensor_tensor(out=pmax[t][:, cols], in0=y_at[:, cols], in1=y_bank[t][:, cols], op=ALU.max)
+        deal_columns(nc.vector.tensor_copy, dealt_codes[2][:], w_codes[2][:].bitcast(U32))
         for t in range(PACK):
-            nc.scalar.copy(out=c[t][:], in_=c_bank[t][:])
-            for lo in (0, HALF):
-                nc.scalar.activation(c_at[t][:, lo : lo + HALF], c[t][:].indirect(entries(n2_t, lo, lo + HALF)), COPY)
+            nc.scalar.copy(out=c[t][:, :S], in_=c_bank[t][:])
+            gather("scalar", c_at[t][:], c[t], n2_t, 0, S)
 
-        def fetch(engine, j, name, source, offsets, tag):
-            lo, hi = CHUNKS[j]
-            fetched = keep.tile([P, PACK, hi - lo], F32, name=f"{name}{j}", tag=tag, align_bytes=64)
-            for t in range(PACK):
-                window = source[t][:].indirect(entries(offsets, lo, hi))
-                if engine == "scalar":
-                    nc.scalar.activation(fetched[:, t, :], window, COPY)
-                else:
-                    nc.vector.tensor_copy(fetched[:, t, :], window)
-            return fetched
+        def chunk_tile(name, j, tag=None):
+            return sbuf(f"{name}{j}", [PACK, CHUNKS[j][1] - CHUNKS[j][0]], F32, tag)
 
-        def second_stage(j, p_at, q_at, tags):
+        def fetch(engine, j, fetched, source, offsets, tiles=range(PACK)):
+            for t in tiles:
+                gather(engine, fetched[:, t, :], source[t], offsets, *CHUNKS[j])
+
+        def times(j, out, source, factor, fetched, tiles=range(PACK)):
             lo, hi = CHUNKS[j]
-            n = hi - lo
-            right = keep.tile([P, PACK, n], F32, name=f"right{j}", tag=tags[0], align_bytes=64)
-            left = keep.tile([P, PACK, n], F32, name=f"left{j}", tag=tags[1], align_bytes=64)
-            z = keep.tile([P, n, PACK], BF16, name=f"z{j}", align_bytes=64)
-            z_codes = keep.tile([P, n], U32, name=f"z_codes{j}", align_bytes=64)
-            z_plane = keep.tile([P, n], U8, name=f"z_plane{j}", align_bytes=64)
-            for t in range(PACK):
-                nc.vector.scalar_tensor_tensor(out=right[:, t, :], in0=qmin[t][:, lo:hi], scalar=minus_gain[:, t : t + 1],
-                                               in1=p_at[:, t, :], op0=ALU.mult, op1=ALU.mult)
-            for t in range(PACK):
-                nc.vector.scalar_tensor_tensor(out=left[:, t, :], in0=pmax[t][:, lo:hi], scalar=gain[:, t : t + 1],
-                                               in1=q_at[:, t, :], op0=ALU.mult, op1=ALU.mult)
-            nc.vector.tensor_tensor(out=z[:].rearrange("p (a i) t -> p a t i", i=4),
-                                    in0=left[:].rearrange("p t (a i) -> p a t i", i=4),
-                                    in1=right[:].rearrange("p t (a i) -> p a t i", i=4), op=ALU.add)
-            nc.vector.quantize_mx(out=z_codes[:].bitcast(FP8X4), scales=z_plane[:], in_=z[:].rearrange("p c t -> p (c t)"))
-            halves = []
+            for t in tiles:
+                nc.vector.scalar_tensor_tensor(out=out[:, t, :], in0=source[t][:, lo:hi], scalar=factor[:, t : t + 1],
+                                               in1=fetched[:, t, :], op0=ALU.mult, op1=ALU.mult)
+
+        def last_product(j, left, right):
+            n = CHUNKS[j][1] - CHUNKS[j][0]
+            z = sbuf(f"z{j}", [n * PACK], BF16)
+            z_codes = sbuf(f"z_codes{j}", [n], U32)
+            z_plane = sbuf(f"z_plane{j}", [n], U8)
+            for lo in range(0, n, PIECE):
+                nc.vector.tensor_tensor(
+                    out=z[:, lo * PACK : (lo + PIECE) * PACK].rearrange("p (a i t) -> p a t i", i=2, t=PACK),
+                    in0=left[:, :, lo : lo + PIECE].rearrange("p t (a i) -> p a t i", i=2),
+                    in1=right[:, :, lo : lo + PIECE].rearrange("p t (a i) -> p a t i", i=2), op=ALU.add)
+            for lo in range(0, n, PIECE):
+                nc.vector.quantize_mx(out=z_codes[:, lo : lo + PIECE].bitcast(FP8X4), scales=z_plane[:, lo : lo + PIECE],
+                                      in_=z[:, lo * PACK : (lo + PIECE) * PACK])
             per_bank = S // n
+            banks = []
             for b in range(PACK // per_bank):
-                bank = psum.tile([P, per_bank, n], F32, name=f"h_bank{j}_{b}", tag=f"bank{j + b}")
+                banks.append(psum.tile([P, per_bank, n], F32, name=f"h_bank{j}_{b}", tag=f"bank{j + b}"))
                 for u in range(per_bank):
-                    product(bank[:, u, :], 2, b * per_bank + u, z_codes[:], z_plane[:])
-                for u in range(0, per_bank, 2):
-                    half = keep.tile([P, 2, n], F32, name=f"h{j}_{len(halves)}", align_bytes=64)
-                    nc.scalar.copy(out=half[:], in_=bank[:, u : u + 2, :])
-                    halves.append(half)
-            return halves
+                    product(banks[b][:, u, :], 2, b * per_bank + u, z_codes[:], z_plane[:])
+            return banks
 
-        def scatter(j, t):
-            lo, hi = CHUNKS[j]
-            nc.vector.tensor_copy(page[t][:].indirect(entries(slot_t, lo, hi)), h[j][t // 2][:, t % 2, :])
+        def scatter(j, t, values):
+            nc.vector.tensor_copy(page[t][:].indirect(entries(slot_t, *CHUNKS[j])), values)
 
-        h = []
-        p_at0 = fetch("vector", 0, "p_at", pmax, n2_t, "p_at0")
+        p_at0, q_at0 = chunk_tile("p_at", 0), chunk_tile("q_at", 0)
+        left0, right0 = chunk_tile("left", 0), chunk_tile("right", 0)
+        fetch("vector", 0, p_at0, pmax, n2_t)
         for t in range(PACK):
             nc.vector.tensor_tensor(out=qmin[t][:], in0=c_at[t][:], in1=c_bank[t][:], op=ALU.min)
-        q_at0 = fetch("scalar", 0, "q_at", qmin, n1_t, "q_at0")
-        h.append(second_stage(0, p_at0, q_at0, ("right0", "left0")))
-        p_at1 = fetch("vector", 1, "p_at", pmax, n2_t, "right0")
-        q_at1 = fetch("scalar", 1, "q_at", qmin, n1_t, "q_at1")
-        h.append(second_stage(1, p_at1, q_at1, ("right1", "left1")))
-        p_at2 = fetch("scalar", 2, "p_at", pmax, n2_t, "z_codes0")
-        q_at2 = fetch("scalar", 2, "q_at", qmin, n1_t, "z_plane0")
+            times(0, right0, qmin, minus_gain, p_at0, [t])
+            fetch("vector", 0, q_at0, qmin, n1_t, [t])
+            times(0, left0, pmax, gain, q_at0, [t])
+        p_at1, q_at1 = chunk_tile("p_at", 1, "y2"), chunk_tile("q_at", 1)
+        fetch("scalar", 1, p_at1, pmax, n2_t)
+        fetch("scalar", 1, q_at1, qmin, n1_t, [0, 1])
+        (bank0,) = last_product(0, left0, right0)
+        h0 = chunk_tile("h", 0)
+        nc.scalar.copy(out=h0[:], in_=bank0[:])
+
+        left1, right1 = chunk_tile("left", 1), chunk_tile("right", 1)
+        times(1, right1, qmin, minus_gain, p_at1)
+        fetch("vector", 1, q_at1, qmin, n1_t, [2, 3])
+        times(1, left1, pmax, gain, q_at1)
+        (bank1,) = last_product(1, left1, right1)
+        p_at2 = chunk_tile("p_at", 2, "z_codes0")
+        fetch("scalar", 2, p_at2, pmax, n2_t)
+        h1_low = sbuf("h1_low", [2, PIECE], F32)
+        nc.scalar.copy(out=h1_low[:], in_=bank1[:, :2, :])
+        q_at2 = chunk_tile("q_at", 2, "z_codes1")
+        fetch("scalar", 2, q_at2, qmin, n1_t)
+
         for t in range(PACK):
-            scatter(0, t)
+            scatter(0, t, h0[:, t, :])
         for t in range(2):
-            scatter(1, t)
-        h.append(second_stage(2, p_at2, q_at2, ("h1_0", "h0_1")))
+            scatter(1, t, h1_low[:, t, :])
+        left2, right2 = chunk_tile("left", 2, "h0"), chunk_tile("right", 2, "h1_low")
+        times(2, right2, qmin, minus_gain, p_at2)
+        times(2, left2, pmax, gain, q_at2)
+        banks2 = last_product(2, left2, right2)
+        h1_high = sbuf("h1_high", [2, PIECE], F32, "h1_low")
+        nc.scalar.copy(out=h1_high[:], in_=bank1[:, 2:, :])
+        h2 = chunk_tile("h", 2)
+        for b in range(2):
+            nc.scalar.copy(out=h2[:, 2 * b : 2 * b + 2, :], in_=banks2[b][:])
         for t in range(2, PACK):
-            scatter(1, t)
+            scatter(1, t, h1_high[:, t - 2, :])
         out_rows = out_0.rearrange("(p t) w -> p t w", t=PACK)
         for t in range(PACK):
-            scatter(2, t)
+            scatter(2, t, h2[:, t, :])
             nc.sync.dma_start(out=out_rows[:, t, :], in_=page[t][:])
 
-        out_plane = keep.tile([P, U], U8, name="out_plane", align_bytes=64)
+        out_plane = sbuf("out_plane", [U], U8)
+        out_codes = sbuf("out_codes", [U], I32)
         out_words = words_of(out_1)
         blocks = U // OUT_CHUNK
-        pairs = [keep.tile([P, 2, OUT_CHUNK, 2], BF16, name=f"pairs{b}", align_bytes=64) for b in range(blocks)]
-        for t in range(PACK):
-            for b in range(blocks):
-                nc.scalar.copy(out=pairs[b][:, t // 2, :, t % 2], in_=page[t][:, b * OUT_CHUNK : (b + 1) * OUT_CHUNK])
-        for b in range(blocks):
+        pairs = sbuf("pairs", [U * PACK], BF16)
+        by_plane = pairs[:].rearrange("p (b u c e) -> p u e b c", b=blocks, u=2, e=2)
+
+        def round_rows(copy, t, b0, b1):
+            copy(out=by_plane[:, t // 2, t % 2, b0:b1, :],
+                 in_=page[t][:, b0 * OUT_CHUNK : b1 * OUT_CHUNK].rearrange("p (b c) -> p b c", c=OUT_CHUNK))
+
+        round_rows(nc.scalar.copy, 0, 0, blocks)
+        round_rows(nc.scalar.copy, 1, 0, blocks)
+        round_rows(nc.scalar.copy, 2, 1, blocks)
+        for b in range(1, blocks):
+            round_rows(nc.scalar.copy, 3, b, b + 1)
+        round_rows(nc.vector.tensor_copy, 3, 0, 1)
+        round_rows(nc.vector.tensor_copy, 2, 0, 1)
+        grouped = [sbuf(f"grouped{b}", [OUT_CHUNK * PACK], BF16) for b in range(blocks)]
+
+        def weave(copy, b):
+            width = OUT_CHUNK * PACK
+            copy(out=grouped[b][:].bitcast(F32).rearrange("p (c u) -> p c u", u=2),
+                 in_=pairs[:, b * width : (b + 1) * width].bitcast(F32).rearrange("p (u c) -> p c u", u=2))
+
+        def quantise_block(b):
             cols = slice(b * OUT_CHUNK, (b + 1) * OUT_CHUNK)
-            grouped = keep.tile([P, OUT_CHUNK * PACK], BF16, name=f"grouped{b}", align_bytes=64)
-            out_codes = keep.tile([P, OUT_CHUNK], I32, name=f"out_codes{b}", align_bytes=64)
-            weave = nc.scalar.copy if b == blocks - 1 else nc.vector.tensor_copy
-            weave(out=grouped[:].bitcast(F32).rearrange("p (a i u) -> p a u i", i=4, u=2),
-                  in_=pairs[b][:].rearrange("p u c e -> p (u c e)").bitcast(F32).rearrange("p (u a i) -> p a u i", u=2, i=4))
-            nc.vector.quantize_mx(out=out_codes[:].bitcast(FP8X4), scales=out_plane[:, cols], in_=grouped[:])
-            nc.sync.dma_start(out=out_words[:, cols], in_=out_codes[:])
+            nc.vector.quantize_mx(out=out_codes[:, cols].bitcast(FP8X4), scales=out_plane[:, cols], in_=grouped[b][:])
+            if b > 0:
+                stored = slice(0 if b == 1 else cols.start, cols.stop)
+                nc.sync.dma_start(out=out_words[:, stored], in_=out_codes[:, stored])
+
+        weave(nc.scalar.copy, blocks - 1)
+        weave(nc.vector.tensor_copy, 0)
+        for b in range(blocks):
+            if b + 1 < blocks - 1:
+                weave(nc.vector.tensor_copy, b + 1)
+            quantise_block(b)
         for q in range(4):
-            nc.scalar.dma_start(out=out_2[0, 4 * q : 4 * q + 4, :].bitcast(I32), in_=out_plane[32 * q : 32 * q + 4, :].bitcast(I32))
+            queue = nc.scalar if q < 2 else nc.sync
+            queue.dma_start(out=out_2[0, 4 * q : 4 * q + 4, :].bitcast(I32), in_=out_plane[32 * q : 32 * q + 4, :].bitcast(I32))

@@ -19,7 +19,7 @@ LIST_ROWS = 16
 HALF = S // 2
 CHUNKS = ((0, 128), (128, 256), (256, 512))
 PIECE = 128
-OUT_CHUNK = 256
+OUT_HALF = U // 2
 FLOPS = 2 * (K * H * S * 2 + H * N * S)
 
 
@@ -77,11 +77,8 @@ def tile_picked_wedge2_none_po_kernel(
         dealt_codes = [sbuf(f"dealt_codes{i}", [H], U32) for i in range(3)]
         dealt_planes = [w1_dealt_plane[:], w23_dealt_plane[:], w23_dealt_plane[4:P, :]]
         gain = keep.tile([P, PACK], F32, name="gain")
-        minus_gain = keep.tile([P, PACK], F32, name="minus_gain")
 
         nc.vector.memset(w23_plane[:].bitcast(I32), 0)
-        nc.gpsimd.dma_start(out=gain[:], in_=gn.rearrange("(p t) o -> p (t o)", t=PACK))
-        nc.scalar.activation(minus_gain[:], gain[:], COPY, scale=-1.0)
         nc.sync.dma_start(offs_t[:], offs)
         load_scale_rows_repeated(nc, x_plane, x_scales)
         nc.sync.dma_start(two_t[:], two)
@@ -94,6 +91,7 @@ def tile_picked_wedge2_none_po_kernel(
         nc.sync.dma_start(n1_t[:], n1)
         nc.sync.dma_start(n2_t[:], n2)
         nc.sync.dma_start(out=w_codes[2][:], in_=words_of(w3_words))
+        nc.sync.dma_start(out=gain[:], in_=gn.rearrange("(p t) o -> p (t o)", t=PACK))
         nc.sync.dma_start(slot_t[:], slot)
         for i in range(2):
             deal_columns(nc.scalar.copy, dealt_codes[i][:], w_codes[i][:].bitcast(U32))
@@ -117,6 +115,7 @@ def tile_picked_wedge2_none_po_kernel(
         y = [sbuf(f"y{t}", [S], F32) for t in range(PACK)]
         c_at = [sbuf(f"c_at{t}", [S], F32) for t in range(PACK)]
         pmax = [sbuf(f"pmax{t}", [S], F32) for t in range(PACK)]
+        gp = [sbuf(f"gp{t}", [S], F32) for t in range(PACK)]
         qmin = [sbuf(f"qmin{t}", [S], F32) for t in range(PACK)]
 
         for t in range(PACK):
@@ -137,7 +136,7 @@ def tile_picked_wedge2_none_po_kernel(
                 nc.vector.tensor_copy(out, window)
 
         for t in range(PACK):
-            nc.scalar.copy(out=y[t][:], in_=y_bank[t][:])
+            nc.scalar.activation(y[t][:], y_bank[t][:], COPY)
         c = []
         for t in range(PACK):
             c.append(sbuf(f"c{t}", [2 * S], F32, f"y{t - 1}" if t else "w23_plane"))
@@ -147,6 +146,8 @@ def tile_picked_wedge2_none_po_kernel(
             for lo in (0, HALF):
                 cols = slice(lo, lo + HALF)
                 nc.vector.tensor_tensor(out=pmax[t][:, cols], in0=y_at[:, cols], in1=y_bank[t][:, cols], op=ALU.max)
+            nc.gpsimd.tensor_scalar(out=gp[t][:], in0=pmax[t][:], scalar1=gain[:, t : t + 1], scalar2=0.0,
+                                    op0=ALU.mult, op1=ALU.add)
         deal_columns(nc.vector.tensor_copy, dealt_codes[2][:], w_codes[2][:].bitcast(U32))
         for t in range(PACK):
             nc.scalar.copy(out=c[t][:, :S], in_=c_bank[t][:])
@@ -159,11 +160,10 @@ def tile_picked_wedge2_none_po_kernel(
             for t in tiles:
                 gather(engine, fetched[:, t, :], source[t], offsets, *CHUNKS[j])
 
-        def times(j, out, source, factor, fetched, tiles=range(PACK)):
+        def times(engine, j, out, source, fetched, tiles=range(PACK)):
             lo, hi = CHUNKS[j]
             for t in tiles:
-                nc.vector.scalar_tensor_tensor(out=out[:, t, :], in0=source[t][:, lo:hi], scalar=factor[:, t : t + 1],
-                                               in1=fetched[:, t, :], op0=ALU.mult, op1=ALU.mult)
+                engine.tensor_tensor(out=out[:, t, :], in0=source[t][:, lo:hi], in1=fetched[:, t, :], op=ALU.mult)
 
         def last_product(j, left, right):
             n = CHUNKS[j][1] - CHUNKS[j][0]
@@ -174,7 +174,7 @@ def tile_picked_wedge2_none_po_kernel(
                 nc.vector.tensor_tensor(
                     out=z[:, lo * PACK : (lo + PIECE) * PACK].rearrange("p (a i t) -> p a t i", i=2, t=PACK),
                     in0=left[:, :, lo : lo + PIECE].rearrange("p t (a i) -> p a t i", i=2),
-                    in1=right[:, :, lo : lo + PIECE].rearrange("p t (a i) -> p a t i", i=2), op=ALU.add)
+                    in1=right[:, :, lo : lo + PIECE].rearrange("p t (a i) -> p a t i", i=2), op=ALU.subtract)
             for lo in range(0, n, PIECE):
                 nc.vector.quantize_mx(out=z_codes[:, lo : lo + PIECE].bitcast(FP8X4), scales=z_plane[:, lo : lo + PIECE],
                                       in_=z[:, lo * PACK : (lo + PIECE) * PACK])
@@ -191,40 +191,48 @@ def tile_picked_wedge2_none_po_kernel(
 
         p_at0, q_at0 = chunk_tile("p_at", 0), chunk_tile("q_at", 0)
         left0, right0 = chunk_tile("left", 0), chunk_tile("right", 0)
-        fetch("vector", 0, p_at0, pmax, n2_t)
+        fetch("vector", 0, p_at0, gp, n2_t)
         for t in range(PACK):
             nc.vector.tensor_tensor(out=qmin[t][:], in0=c_at[t][:], in1=c_bank[t][:], op=ALU.min)
-            times(0, right0, qmin, minus_gain, p_at0, [t])
             fetch("vector", 0, q_at0, qmin, n1_t, [t])
-            times(0, left0, pmax, gain, q_at0, [t])
+            times(nc.gpsimd, 0, right0, qmin, p_at0, [t])
+            times(nc.gpsimd, 0, left0, gp, q_at0, [t])
         p_at1, q_at1 = chunk_tile("p_at", 1, "y2"), chunk_tile("q_at", 1)
-        fetch("scalar", 1, p_at1, pmax, n2_t)
-        fetch("scalar", 1, q_at1, qmin, n1_t, [0, 1])
+        fetch("scalar", 1, p_at1, gp, n2_t)
+        fetch("scalar", 1, q_at1, qmin, n1_t, range(2))
         (bank0,) = last_product(0, left0, right0)
+        p_at2_first = chunk_tile("p_at_first", 2, "q_at0")
+        fetch("scalar", 2, p_at2_first, gp, n2_t, range(1))
         h0 = chunk_tile("h", 0)
         nc.scalar.copy(out=h0[:], in_=bank0[:])
 
-        left1, right1 = chunk_tile("left", 1), chunk_tile("right", 1)
-        times(1, right1, qmin, minus_gain, p_at1)
-        fetch("vector", 1, q_at1, qmin, n1_t, [2, 3])
-        times(1, left1, pmax, gain, q_at1)
+        left1, right1 = chunk_tile("left", 1, "left0"), chunk_tile("right", 1, "right0")
+        fetch("vector", 1, q_at1, qmin, n1_t, range(2, PACK))
+        times(nc.vector, 1, right1, qmin, p_at1)
+        times(nc.vector, 1, left1, gp, q_at1)
         (bank1,) = last_product(1, left1, right1)
         p_at2 = chunk_tile("p_at", 2, "z_codes0")
-        fetch("scalar", 2, p_at2, pmax, n2_t)
-        h1_low = sbuf("h1_low", [2, PIECE], F32)
-        nc.scalar.copy(out=h1_low[:], in_=bank1[:, :2, :])
+        fetch("scalar", 2, p_at2, gp, n2_t, range(1, PACK))
+        h1 = sbuf("h1", [2, PIECE], F32)
+        nc.scalar.copy(out=h1[:], in_=bank1[:, :2, :])
         q_at2 = chunk_tile("q_at", 2, "z_codes1")
-        fetch("scalar", 2, q_at2, qmin, n1_t)
+        fetch("scalar", 2, q_at2, qmin, n1_t, range(3))
 
         for t in range(PACK):
             scatter(0, t, h0[:, t, :])
+        left2, right2 = chunk_tile("left", 2), chunk_tile("right", 2, "z1")
+        for t in range(PACK):
+            times(nc.gpsimd, 2, right2, qmin, p_at2_first if t < 1 else p_at2, [t])
+        q_at2v = chunk_tile("q_atv", 2, "h0")
+        fetch("vector", 2, q_at2v, qmin, n1_t, range(3, PACK))
         for t in range(2):
-            scatter(1, t, h1_low[:, t, :])
-        left2, right2 = chunk_tile("left", 2, "h0"), chunk_tile("right", 2, "h1_low")
-        times(2, right2, qmin, minus_gain, p_at2)
-        times(2, left2, pmax, gain, q_at2)
+            scatter(1, t, h1[:, t, :])
+        for t in (0, 3, 1):
+            times(nc.gpsimd, 2, left2, gp, q_at2 if t < 3 else q_at2v, [t])
+        for t in (2,):
+            times(nc.vector, 2, left2, gp, q_at2 if t < 3 else q_at2v, [t])
         banks2 = last_product(2, left2, right2)
-        h1_high = sbuf("h1_high", [2, PIECE], F32, "h1_low")
+        h1_high = sbuf("h1_high", [PACK - 2, PIECE], F32, "left2")
         nc.scalar.copy(out=h1_high[:], in_=bank1[:, 2:, :])
         h2 = chunk_tile("h", 2)
         for b in range(2):
@@ -239,41 +247,24 @@ def tile_picked_wedge2_none_po_kernel(
         out_plane = sbuf("out_plane", [U], U8)
         out_codes = sbuf("out_codes", [U], I32)
         out_words = words_of(out_1)
-        blocks = U // OUT_CHUNK
         pairs = sbuf("pairs", [U * PACK], BF16)
-        by_plane = pairs[:].rearrange("p (b u c e) -> p u e b c", b=blocks, u=2, e=2)
+        by_plane = pairs[:].rearrange("p (b u c e) -> p u e b c", b=2, u=2, e=2)
 
         def round_rows(copy, t, b0, b1):
             copy(out=by_plane[:, t // 2, t % 2, b0:b1, :],
-                 in_=page[t][:, b0 * OUT_CHUNK : b1 * OUT_CHUNK].rearrange("p (b c) -> p b c", c=OUT_CHUNK))
+                 in_=page[t][:, b0 * OUT_HALF : b1 * OUT_HALF].rearrange("p (b c) -> p b c", c=OUT_HALF))
 
-        round_rows(nc.scalar.copy, 0, 0, blocks)
-        round_rows(nc.scalar.copy, 1, 0, blocks)
-        round_rows(nc.scalar.copy, 2, 1, blocks)
-        for b in range(1, blocks):
-            round_rows(nc.scalar.copy, 3, b, b + 1)
-        round_rows(nc.vector.tensor_copy, 3, 0, 1)
-        round_rows(nc.vector.tensor_copy, 2, 0, 1)
-        grouped = [sbuf(f"grouped{b}", [OUT_CHUNK * PACK], BF16) for b in range(blocks)]
-
-        def weave(copy, b):
-            width = OUT_CHUNK * PACK
-            copy(out=grouped[b][:].bitcast(F32).rearrange("p (c u) -> p c u", u=2),
-                 in_=pairs[:, b * width : (b + 1) * width].bitcast(F32).rearrange("p (u c) -> p c u", u=2))
-
-        def quantise_block(b):
-            cols = slice(b * OUT_CHUNK, (b + 1) * OUT_CHUNK)
-            nc.vector.quantize_mx(out=out_codes[:, cols].bitcast(FP8X4), scales=out_plane[:, cols], in_=grouped[b][:])
-            if b > 0:
-                stored = slice(0 if b == 1 else cols.start, cols.stop)
-                nc.sync.dma_start(out=out_words[:, stored], in_=out_codes[:, stored])
-
-        weave(nc.scalar.copy, blocks - 1)
-        weave(nc.vector.tensor_copy, 0)
-        for b in range(blocks):
-            if b + 1 < blocks - 1:
-                weave(nc.vector.tensor_copy, b + 1)
-            quantise_block(b)
+        round_rows(nc.scalar.copy, 0, 0, 2)
+        round_rows(nc.scalar.copy, 1, 0, 2)
+        for b, copy in enumerate((nc.vector.tensor_copy, nc.scalar.copy)):
+            cols = slice(b * OUT_HALF, (b + 1) * OUT_HALF)
+            round_rows(copy, 2, b, b + 1)
+            round_rows(copy, 3, b, b + 1)
+            grouped = sbuf(f"grouped{b}", [OUT_HALF * PACK], BF16)
+            copy(out=grouped[:].bitcast(F32).rearrange("p (c u) -> p c u", u=2),
+                 in_=pairs[:, cols.start * PACK : cols.stop * PACK].bitcast(F32).rearrange("p (u c) -> p c u", u=2))
+            nc.vector.quantize_mx(out=out_codes[:, cols].bitcast(FP8X4), scales=out_plane[:, cols], in_=grouped[:])
+            nc.sync.dma_start(out=out_words[:, cols], in_=out_codes[:, cols])
         for q in range(4):
             queue = nc.scalar if q < 2 else nc.sync
             queue.dma_start(out=out_2[0, 4 * q : 4 * q + 4, :].bitcast(I32), in_=out_plane[32 * q : 32 * q + 4, :].bitcast(I32))

from contextlib import ExitStack

import concourse.mybir as mybir

F32 = mybir.dt.float32
BF16 = mybir.dt.bfloat16
I32 = mybir.dt.int32
U32 = mybir.dt.uint32
U16 = mybir.dt.uint16
U8 = mybir.dt.uint8
FP8X4 = mybir.dt.float8_e4m3fn_x4
ALU = mybir.AluOpType
COPY = mybir.ActivationFunctionType.Copy

P = 128
PACK = 4
K, T, S, N, H, U = 512, 2048, 512, 512, 512, 1024
LIST_ROWS = 16
HALF = S // 2
CHUNKS = ((0, 128), (128, 256), (256, 512))
PIECE = 128
OUT_HALF = U // 2
FLOPS = 2 * (K * H * S * 2 + H * N * S)


def entries(offsets, lo, hi):
    return offsets[:, lo // LIST_ROWS : hi // LIST_ROWS]


def load_scale_rows_repeated(nc, plane, scales):
    for q in range(4):
        rows = scales[0, 4 * q : 4 * q + 4, :].bitcast(I32)
        nc.sync.dma_start(out=plane[32 * q : 32 * q + 32, :].bitcast(I32),
                          in_=rows.unsqueeze(0).to_broadcast([8, 4, rows.shape[1]]))


def load_scale_rows(nc, plane, first, scales):
    for q in range(4):
        nc.sync.dma_start(out=plane[32 * q + first : 32 * q + first + 4, :].bitcast(I32),
                          in_=scales[0, 4 * q : 4 * q + 4, :].bitcast(I32))


def words_of(packed):
    return packed[0].rearrange("p c r -> p (c r)").bitcast(I32)


def deal_columns(copy, dealt, natural):
    copy(out=dealt.rearrange("p (t m) -> p t m", t=PACK), in_=natural.rearrange("p (m t) -> p t m", t=PACK))


def tile_picked_wedge2_none_po_kernel(
    tc, x_words, x_scales, w1_words, w1_scales, w2_words, w2_scales, gn, w3_words, w3_scales, mem,
    offs, two, n1, n2, slot, out_0, out_1, out_2,
):
    nc = tc.nc
    with ExitStack() as ctx:
        lists = ctx.enter_context(tc.tile_pool(name="lists", bufs=1))
        keep = ctx.enter_context(tc.tile_pool(name="keep", bufs=1))
        psum = ctx.enter_context(tc.psum_pool(name="psum", bufs=1))

        def sbuf(name, shape, dtype, tag=None):
            return keep.tile([P] + shape, dtype, name=name, tag=tag or name, align_bytes=64)

        offs_t = lists.tile([P, S // LIST_ROWS], U16, name="offs_t")
        two_t = lists.tile([P, S // LIST_ROWS], U16, name="two_t")
        n1_t = lists.tile([P, S // LIST_ROWS], U16, name="n1_t")
        n2_t = lists.tile([P, S // LIST_ROWS], U16, name="n2_t")
        slot_t = lists.tile([P, S // LIST_ROWS], U16, name="slot_t")

        x_plane = sbuf("x_plane", [T], U8)
        x_codes = sbuf("x_codes", [T], I32)
        w1_plane = sbuf("w1_plane", [H], U8)
        w23_plane = sbuf("w23_plane", [H], U8)
        w1_dealt_plane = sbuf("w1_dealt_plane", [H], U8)
        w23_dealt_plane = sbuf("w23_dealt_plane", [H], U8)
        w_codes = [sbuf(f"w_codes{i}", [H], I32) for i in range(3)]
        dealt_codes = [sbuf(f"dealt_codes{i}", [H], U32) for i in range(3)]
        dealt_planes = [w1_dealt_plane[:], w23_dealt_plane[:], w23_dealt_plane[4:P, :]]
        gain = keep.tile([P, PACK], F32, name="gain")

        nc.vector.memset(w23_plane[:].bitcast(I32), 0)
        nc.sync.dma_start(offs_t[:], offs)
        load_scale_rows_repeated(nc, x_plane, x_scales)
        nc.sync.dma_start(two_t[:], two)
        nc.sync.dma_start(out=x_codes[:], in_=words_of(x_words))
        nc.sync.dma_start(out=w_codes[0][:], in_=words_of(w1_words))
        load_scale_rows_repeated(nc, w1_plane, w1_scales)
        load_scale_rows(nc, w23_plane, 0, w2_scales)
        load_scale_rows(nc, w23_plane, 4, w3_scales)
        nc.sync.dma_start(out=w_codes[1][:], in_=words_of(w2_words))
        nc.sync.dma_start(n1_t[:], n1)
        nc.sync.dma_start(n2_t[:], n2)
        nc.sync.dma_start(out=w_codes[2][:], in_=words_of(w3_words))
        nc.sync.dma_start(out=gain[:], in_=gn.rearrange("(p t) o -> p (t o)", t=PACK))
        nc.sync.dma_start(slot_t[:], slot)
        for i in range(2):
            deal_columns(nc.scalar.copy, dealt_codes[i][:], w_codes[i][:].bitcast(U32))

        picked_plane = [sbuf(f"picked_plane{i}", [S], U8) for i in range(2)]
        picked_codes = []
        for i, offsets in enumerate((offs_t, two_t)):
            nc.vector.tensor_copy(picked_plane[i][:], x_plane[:].indirect(offsets[:]))
        for i, offsets in enumerate((offs_t, two_t)):
            picked_codes.append(sbuf(f"picked_codes{i}", [S], U32, "w1_plane" if i else None))
            nc.vector.tensor_copy(picked_codes[i][:], x_codes[:].bitcast(U32).indirect(offsets[:]))
            deal_columns(nc.vector.tensor_copy, (w1_dealt_plane, w23_dealt_plane)[i][:], (w1_plane, w23_plane)[i][:])

        def product(bank, i, t, codes, plane):
            cols = slice(P * t, P * (t + 1))
            nc.tensor.matmul_mx(out=bank, lhsT=dealt_codes[i][:, cols].bitcast(FP8X4), lhsT_scale=dealt_planes[i][:, cols],
                                rhs=codes.bitcast(FP8X4), rhs_scale=plane, start=True, stop=True)

        y_bank = [psum.tile([P, S], F32, name=f"y_bank{t}", tag=f"bank{t}") for t in range(PACK)]
        c_bank = [psum.tile([P, S], F32, name=f"c_bank{t}", tag=f"bank{PACK + t}") for t in range(PACK)]
        y = [sbuf(f"y{t}", [S], F32) for t in range(PACK)]
        c_at = [sbuf(f"c_at{t}", [S], F32) for t in range(PACK)]
        pmax = [sbuf(f"pmax{t}", [S], F32) for t in range(PACK)]
        gp = [sbuf(f"gp{t}", [S], F32) for t in range(PACK)]
        qmin = [sbuf(f"qmin{t}", [S], F32) for t in range(PACK)]

        for t in range(PACK):
            product(y_bank[t][:], 0, t, picked_codes[0][:], picked_plane[0][:])
        for t in range(PACK):
            product(c_bank[t][:], 1, t, picked_codes[1][:], picked_plane[1][:])
        mem_rows = mem.rearrange("(p t) w -> p t w", t=PACK)
        page = []
        for t, tag in enumerate(("x_plane", "picked_codes0", "x_codes", "w1_plane")):
            page.append(sbuf(f"page{t}", [U], F32, tag))
            nc.sync.dma_start(out=page[t][:], in_=mem_rows[:, t, :])

        def gather(engine, out, source, offsets, lo, hi):
            window = source[:].indirect(entries(offsets, lo, hi))
            if engine == "scalar":
                nc.scalar.activation(out, window, COPY)
            else:
                nc.vector.tensor_copy(out, window)

        for t in range(PACK):
            nc.scalar.activation(y[t][:], y_bank[t][:], COPY)
        c = []
        for t in range(PACK):
            c.append(sbuf(f"c{t}", [2 * S], F32, f"y{t - 1}" if t else "w23_plane"))
            y_at = c[t][:, S:]
            for lo in (0, HALF):
                gather("vector", y_at[:, lo : lo + HALF], y[t], n1_t, lo, lo + HALF)
            for lo in (0, HALF):
                cols = slice(lo, lo + HALF)
                nc.vector.tensor_tensor(out=pmax[t][:, cols], in0=y_at[:, cols], in1=y_bank[t][:, cols], op=ALU.max)
            nc.gpsimd.tensor_scalar(out=gp[t][:], in0=pmax[t][:], scalar1=gain[:, t : t + 1], scalar2=0.0,
                                    op0=ALU.mult, op1=ALU.add)
        deal_columns(nc.vector.tensor_copy, dealt_codes[2][:], w_codes[2][:].bitcast(U32))
        for t in range(PACK):
            nc.scalar.copy(out=c[t][:, :S], in_=c_bank[t][:])
            gather("scalar", c_at[t][:], c[t], n2_t, 0, S)

        def chunk_tile(name, j, tag=None):
            return sbuf(f"{name}{j}", [PACK, CHUNKS[j][1] - CHUNKS[j][0]], F32, tag)

        def fetch(engine, j, fetched, source, offsets, tiles=range(PACK)):
            for t in tiles:
                gather(engine, fetched[:, t, :], source[t], offsets, *CHUNKS[j])

        def times(engine, j, out, source, fetched, tiles=range(PACK)):
            lo, hi = CHUNKS[j]
            for t in tiles:
                engine.tensor_tensor(out=out[:, t, :], in0=source[t][:, lo:hi], in1=fetched[:, t, :], op=ALU.mult)

        def last_product(j, left, right):
            n = CHUNKS[j][1] - CHUNKS[j][0]
            z = sbuf(f"z{j}", [n * PACK], BF16)
            z_codes = sbuf(f"z_codes{j}", [n], U32)
            z_plane = sbuf(f"z_plane{j}", [n], U8)
            for lo in range(0, n, PIECE):
                nc.vector.tensor_tensor(
                    out=z[:, lo * PACK : (lo + PIECE) * PACK].rearrange("p (a i t) -> p a t i", i=2, t=PACK),
                    in0=left[:, :, lo : lo + PIECE].rearrange("p t (a i) -> p a t i", i=2),
                    in1=right[:, :, lo : lo + PIECE].rearrange("p t (a i) -> p a t i", i=2), op=ALU.subtract)
            for lo in range(0, n, PIECE):
                nc.vector.quantize_mx(out=z_codes[:, lo : lo + PIECE].bitcast(FP8X4), scales=z_plane[:, lo : lo + PIECE],
                                      in_=z[:, lo * PACK : (lo + PIECE) * PACK])
            per_bank = S // n
            banks = []
            for b in range(PACK // per_bank):
                banks.append(psum.tile([P, per_bank, n], F32, name=f"h_bank{j}_{b}", tag=f"bank{j + b}"))
                for u in range(per_bank):
                    product(banks[b][:, u, :], 2, b * per_bank + u, z_codes[:], z_plane[:])
            return banks

        def scatter(j, t, values):
            nc.vector.tensor_copy(page[t][:].indirect(entries(slot_t, *CHUNKS[j])), values)

        p_at0, q_at0 = chunk_tile("p_at", 0), chunk_tile("q_at", 0)
        left0, right0 = chunk_tile("left", 0), chunk_tile("right", 0)
        fetch("vector", 0, p_at0, gp, n2_t)
        for t in range(PACK):
            nc.vector.tensor_tensor(out=qmin[t][:], in0=c_at[t][:], in1=c_bank[t][:], op=ALU.min)
            fetch("vector", 0, q_at0, qmin, n1_t, [t])
            times(nc.gpsimd, 0, right0, qmin, p_at0, [t])
            times(nc.gpsimd, 0, left0, gp, q_at0, [t])
        p_at1, q_at1 = chunk_tile("p_at", 1, "y2"), chunk_tile("q_at", 1)
        fetch("scalar", 1, p_at1, gp, n2_t)
        fetch("scalar", 1, q_at1, qmin, n1_t, range(2))
        (bank0,) = last_product(0, left0, right0)
        p_at2_first = chunk_tile("p_at_first", 2, "q_at0")
        fetch("scalar", 2, p_at2_first, gp, n2_t, range(1))
        h0 = chunk_tile("h", 0)
        nc.scalar.copy(out=h0[:], in_=bank0[:])

        left1, right1 = chunk_tile("left", 1, "left0"), chunk_tile("right", 1, "right0")
        fetch("vector", 1, q_at1, qmin, n1_t, range(2, PACK))
        times(nc.vector, 1, right1, qmin, p_at1)
        times(nc.vector, 1, left1, gp, q_at1)
        (bank1,) = last_product(1, left1, right1)
        p_at2 = chunk_tile("p_at", 2, "z_codes0")
        fetch("scalar", 2, p_at2, gp, n2_t, range(1, PACK))
        h1 = sbuf("h1", [2, PIECE], F32)
        nc.scalar.copy(out=h1[:], in_=bank1[:, :2, :])
        q_at2 = chunk_tile("q_at", 2, "z_codes1")
        fetch("scalar", 2, q_at2, qmin, n1_t, range(3))

        for t in range(PACK):
            scatter(0, t, h0[:, t, :])
        left2, right2 = chunk_tile("left", 2), chunk_tile("right", 2, "z1")
        for t in range(PACK):
            times(nc.gpsimd, 2, right2, qmin, p_at2_first if t < 1 else p_at2, [t])
        q_at2v = chunk_tile("q_atv", 2, "h0")
        fetch("vector", 2, q_at2v, qmin, n1_t, range(3, PACK))
        for t in range(2):
            scatter(1, t, h1[:, t, :])
        for t in (0, 3, 1):
            times(nc.gpsimd, 2, left2, gp, q_at2 if t < 3 else q_at2v, [t])
        for t in (2,):
            times(nc.vector, 2, left2, gp, q_at2 if t < 3 else q_at2v, [t])
        banks2 = last_product(2, left2, right2)
        h1_high = sbuf("h1_high", [PACK - 2, PIECE], F32, "left2")
        nc.scalar.copy(out=h1_high[:], in_=bank1[:, 2:, :])
        h2 = chunk_tile("h", 2)
        for b in range(2):
            nc.scalar.copy(out=h2[:, 2 * b : 2 * b + 2, :], in_=banks2[b][:])
        for t in range(2, PACK):
            scatter(1, t, h1_high[:, t - 2, :])
        out_rows = out_0.rearrange("(p t) w -> p t w", t=PACK)
        for t in range(PACK):
            scatter(2, t, h2[:, t, :])
            nc.sync.dma_start(out=out_rows[:, t, :], in_=page[t][:])

        out_plane = sbuf("out_plane", [U], U8)
        out_codes = sbuf("out_codes", [U], I32)
        out_words = words_of(out_1)
        pairs = sbuf("pairs", [U * PACK], BF16)
        by_plane = pairs[:].rearrange("p (b u c e) -> p u e b c", b=2, u=2, e=2)

        def round_rows(copy, t, b0, b1):
            copy(out=by_plane[:, t // 2, t % 2, b0:b1, :],
                 in_=page[t][:, b0 * OUT_HALF : b1 * OUT_HALF].rearrange("p (b c) -> p b c", c=OUT_HALF))

        round_rows(nc.scalar.copy, 0, 0, 2)
        round_rows(nc.scalar.copy, 1, 0, 2)
        for b, copy in enumerate((nc.vector.tensor_copy, nc.scalar.copy)):
            cols = slice(b * OUT_HALF, (b + 1) * OUT_HALF)
            round_rows(copy, 2, b, b + 1)
            round_rows(copy, 3, b, b + 1)
            grouped = sbuf(f"grouped{b}", [OUT_HALF * PACK], BF16)
            copy(out=grouped[:].bitcast(F32).rearrange("p (c u) -> p c u", u=2),
                 in_=pairs[:, cols.start * PACK : cols.stop * PACK].bitcast(F32).rearrange("p (u c) -> p c u", u=2))
            nc.vector.quantize_mx(out=out_codes[:, cols].bitcast(FP8X4), scales=out_plane[:, cols], in_=grouped[:])
            nc.sync.dma_start(out=out_words[:, cols], in_=out_codes[:, cols])
        for q in range(4):
            queue = nc.scalar if q < 2 else nc.sync
            queue.dma_start(out=out_2[0, 4 * q : 4 * q + 4, :].bitcast(I32), in_=out_plane[32 * q : 32 * q + 4, :].bitcast(I32))
